import numpy as np
import ml_dtypes

BF16 = ml_dtypes.bfloat16


def bf(x):
    return np.asarray(x, np.float32).astype(BF16)


def f32(x):
    return np.asarray(x, np.float32)


def f64(x):
    return np.asarray(x).astype(np.float64)


def striped(idx):
    return np.concatenate([l.reshape(-1, 16).T for l in idx])


def rows(idx, k):
    return np.tile(np.repeat(idx, 16, axis=0), (k // (16 * 8), 1))


def look(tab, idx):
    return np.take_along_axis(f64(tab), rows(idx, len(tab)), axis=1)


K, S, V, N, M = 256, 2048, 1536, 1536, 128


def gelu_tanh(v):
    return 0.5 * v * (1.0 + np.tanh(np.sqrt(2.0 / np.pi) * (v + 0.044715 * v**3)))


def setup_inputs():
    return {"tab": bf(np.random.standard_normal((K, S))), "w": bf(np.random.standard_normal((K, M)) / np.sqrt(K)), "b": f32(0.5 * np.random.standard_normal((M, 1))), "offs": striped(np.random.randint(0, S, (8, N)))}


def reference(tab, w, b, offs):
    idx = np.stack([g.T.reshape(-1) for g in np.split(offs, 8)])
    t = look(tab, idx)
    x = t
    y = f64(w).T @ x
    return gelu_tanh(y + f64(b))

@@ -1,0 +1,47 @@
+import concourse.mybir as mybir
+
+P = 128
+CHUNK = 512
+ENTRIES_PER_COLUMN = 16
+
+BF16, F32, U16 = mybir.dt.bfloat16, mybir.dt.float32, mybir.dt.uint16
+GELU_TANH = mybir.ActivationFunctionType.Gelu_apprx_tanh
+
+FLOPS = 2 * 256 * 128 * 1536
+
+
+def tile_lookup_dec_copy_gelu_kernel(tc, tab, w, b, offs, out):
+    nc = tc.nc
+    rows, columns = tab.shape
+    m = w.shape[1]
+    n = out.shape[1]
+    blocks = rows // P
+    chunks = n // CHUNK
+    offs_per_chunk = CHUNK // ENTRIES_PER_COLUMN
+
+    with (
+        tc.tile_pool(name="held", bufs=1) as held,
+        tc.psum_pool(name="psum", bufs=1) as psum,
+    ):
+        offsets = held.tile([P, n // ENTRIES_PER_COLUMN], U16, name="offsets")
+        nc.sync.dma_start(offsets[:], offs)
+        windows = []
+        for k in range(blocks):
+            window = held.tile([P, columns], BF16, name=f"window{k}")
+            nc.sync.dma_start(window[:], tab[k * P : (k + 1) * P, :])
+            windows.append(window)
+        weights = held.tile([P, blocks, m], BF16, name="weights")
+        nc.sync.dma_start(weights[:], w.rearrange("(k p) m -> p k m", p=P))
+        bias = held.tile([m, 1], F32, name="bias")
+        nc.sync.dma_start(bias[:], b)
+
+        for c in range(chunks):
+            chunk_offsets = offsets[:, c * offs_per_chunk : (c + 1) * offs_per_chunk]
+            y = psum.tile([m, CHUNK], F32, name=f"y{c}")
+            for k in range(blocks):
+                x = held.tile([P, CHUNK], BF16, name=f"x{c}_{k}")
+                nc.vector.tensor_copy(x[:], windows[k][:].indirect(chunk_offsets))
+                nc.tensor.matmul(y[:], weights[:, k, :], x[:], start=(k == 0), stop=(k == blocks - 1))
+            activated = held.tile([m, CHUNK], F32, name=f"activated{c}")
+            nc.scalar.activation(activated[:], y[:], GELU_TANH, bias=bias[:, 0:1])
+            nc.sync.dma_start(out[:, c * CHUNK : (c + 1) * CHUNK], activated[:])

@@ -35,6 +35,10 @@ def tile_lookup_dec_copy_gelu_kernel(tc, tab, w, b, offs, out):
         bias = held.tile([m, 1], F32, name="bias")
         nc.sync.dma_start(bias[:], b)
 
+        warm_up = held.tile([P, 2], F32, name="warm_up")
+        nc.vector.memset(warm_up[:], 0.0)
+        nc.scalar.activation(warm_up[:, 1:2], warm_up[:, 0:1], GELU_TANH)
+
         for c in range(chunks):
             chunk_offsets = offsets[:, c * offs_per_chunk : (c + 1) * offs_per_chunk]
             y = psum.tile([m, CHUNK], F32, name=f"y{c}")

import concourse.mybir as mybir

P = 128
CHUNK = 512
ENTRIES_PER_COLUMN = 16

BF16, F32, U16 = mybir.dt.bfloat16, mybir.dt.float32, mybir.dt.uint16
GELU_TANH = mybir.ActivationFunctionType.Gelu_apprx_tanh

FLOPS = 2 * 256 * 128 * 1536


def tile_lookup_dec_copy_gelu_kernel(tc, tab, w, b, offs, out):
    nc = tc.nc
    rows, columns = tab.shape
    m = w.shape[1]
    n = out.shape[1]
    blocks = rows // P
    chunks = n // CHUNK
    offs_per_chunk = CHUNK // ENTRIES_PER_COLUMN

    with (
        tc.tile_pool(name="held", bufs=1) as held,
        tc.psum_pool(name="psum", bufs=1) as psum,
    ):
        offsets = held.tile([P, n // ENTRIES_PER_COLUMN], U16, name="offsets")
        nc.sync.dma_start(offsets[:], offs)
        windows = []
        for k in range(blocks):
            window = held.tile([P, columns], BF16, name=f"window{k}")
            nc.sync.dma_start(window[:], tab[k * P : (k + 1) * P, :])
            windows.append(window)
        weights = held.tile([P, blocks, m], BF16, name="weights")
        nc.sync.dma_start(weights[:], w.rearrange("(k p) m -> p k m", p=P))
        bias = held.tile([m, 1], F32, name="bias")
        nc.sync.dma_start(bias[:], b)

        warm_up = held.tile([P, 2], F32, name="warm_up")
        nc.vector.memset(warm_up[:], 0.0)
        nc.scalar.activation(warm_up[:, 1:2], warm_up[:, 0:1], GELU_TANH)

        for c in range(chunks):
            chunk_offsets = offsets[:, c * offs_per_chunk : (c + 1) * offs_per_chunk]
            y = psum.tile([m, CHUNK], F32, name=f"y{c}")
            for k in range(blocks):
                x = held.tile([P, CHUNK], BF16, name=f"x{c}_{k}")
                nc.vector.tensor_copy(x[:], windows[k][:].indirect(chunk_offsets))
                nc.tensor.matmul(y[:], weights[:, k, :], x[:], start=(k == 0), stop=(k == blocks - 1))
            activated = held.tile([m, CHUNK], F32, name=f"activated{c}")
            nc.scalar.activation(activated[:], y[:], GELU_TANH, bias=bias[:, 0:1])
            nc.sync.dma_start(out[:, c * CHUNK : (c + 1) * CHUNK], activated[:])
